import numpy as np
import ml_dtypes


def mxq(x, axis, fmt="e4m3"):
    dtype, down = {"e4m3": (ml_dtypes.float8_e4m3fn, 7), "e5m2": (ml_dtypes.float8_e5m2, 14)}[fmt]
    v = np.moveaxis(np.asarray(x, np.float32).astype(ml_dtypes.bfloat16).astype(np.float64), axis, -1)
    blocks = v.reshape(v.shape[:-1] + (-1, 32))
    amax = np.abs(blocks).max(-1, keepdims=True)
    byte = np.maximum(np.where(amax > 0, np.frexp(amax)[1] - 1 + 127, 0) - down, 1)
    scale = np.exp2(byte - 127.0)
    codes = (blocks / scale).astype(np.float32).astype(dtype).astype(np.float64)
    return np.moveaxis((codes * scale).reshape(v.shape), -1, axis)


WIDE = False


def mx_kscale(k):
    if not WIDE:
        return np.ones(k)
    levels = np.array([30, -30])
    if k % 512:
        return np.exp2(np.random.permutation(np.resize(levels, k // 32))).repeat(32)
    a = np.empty((k // 512, 16))
    for p in range(k // 512):
        a[p, :8] = np.random.permutation(np.resize(levels, 8))
        for g in range(8):
            far = levels[np.abs(levels - a[p, g]) >= 10]
            a[p, g + 8] = far[np.random.randint(len(far))]
    return np.exp2(a.ravel()).repeat(32)


BF16 = ml_dtypes.bfloat16


def bf(x):
    return np.asarray(x, np.float32).astype(BF16)


def f64(x):
    return np.asarray(x).astype(np.float64)


E2M1 = np.array([0.0, 0.5, 1.0, 1.5, 2.0, 3.0, 4.0, 6.0, -0.0, -0.5, -1.0, -1.5, -2.0, -3.0, -4.0, -6.0])


def pack_weight(w, fmt):
    k, n = w.shape
    w = f64(bf(w)).reshape(k // 32, 32, n)
    amax = np.abs(w).max(1)
    if fmt in ("e4m3", "e5m2"):
        byte = np.frexp(amax)[1] - 1 + 127 - (7 if fmt == "e4m3" else 14)
    else:
        mant, ex = np.frexp(amax / 6.0)
        byte = np.where(mant > 0.5, ex, ex - 1) + 127
    byte = np.clip(np.where(amax > 0, byte, 1), 1, 254)
    scaled = (w * np.exp2(127.0 - byte)[:, None, :]).reshape(k, n).astype(np.float32)
    by_word = np.ascontiguousarray(scaled.reshape(k // 512, 128, 4, n).transpose(0, 1, 3, 2))
    if fmt in ("e4m3", "e5m2"):
        words = by_word.astype(ml_dtypes.float8_e4m3fn if fmt == "e4m3" else ml_dtypes.float8_e5m2).view(np.uint8)
    else:
        c = by_word.astype(ml_dtypes.float4_e2m1fn).view(np.uint8) & 0xF
        words = c[..., 0::2] | (c[..., 1::2] << 4)
    return np.ascontiguousarray(words), np.ascontiguousarray(byte.astype(np.uint8).reshape(k // 512, 16, n))


def unpack_weight(words, scales, fmt):
    g, p, n, _ = words.shape
    if fmt in ("e4m3", "e5m2"):
        vals = np.ascontiguousarray(words).view(ml_dtypes.float8_e4m3fn if fmt == "e4m3" else ml_dtypes.float8_e5m2).astype(np.float64)
    else:
        nib = np.empty((g, p, n, 4), np.uint8)
        nib[..., 0::2] = words & 0xF
        nib[..., 1::2] = words >> 4
        vals = E2M1[nib]
    vals = vals * np.repeat(np.exp2(scales.astype(np.float64) - 127.0), 8, axis=1)[..., None]
    return vals.transpose(0, 1, 3, 2).reshape(g * 512, n)


M, N, R = 2048, 1536, 512

BETA = 0.5


def setup_inputs():
    s = mx_kscale(M)
    t = mx_kscale(N)
    G = np.random.standard_normal((M, N)) * np.exp(0.5 * np.random.standard_normal((M, N)))
    g_words, g_scales = pack_weight(G * s[:, None], "e5m2")
    basis = np.linalg.qr(np.random.standard_normal((M, R)))[0]
    return {"g_words": g_words,
            "g_scales": g_scales,
            "left": bf(basis / s[:, None]),
            "right_prev": bf(np.random.standard_normal((N, R))),
            "gain": bf((1 + 0.1 * np.random.standard_normal(N)) * t),
            "h": bf(np.random.standard_normal((M, N)) / np.sqrt(N) / t)}


def reference(g_words, g_scales, left, right_prev, gain, h):
    g = unpack_weight(g_words, g_scales, "e5m2")
    right = g.T @ mxq(f64(left), 0, "e4m3")
    right = right + BETA * f64(right_prev)
    scaled = right * f64(gain)[:, None]
    sketch = mxq(f64(h), 1, "e4m3") @ mxq(scaled, 0, "e5m2")
    return right, sketch

@@ -1,0 +1,300 @@
+from contextlib import ExitStack
+
+import concourse.mybir as mybir
+from concourse.masks import make_identity
+
+M, N, R = 2048, 1536, 512
+BETA = 0.5
+
+F32 = mybir.dt.float32
+BF16 = mybir.dt.bfloat16
+I32 = mybir.dt.int32
+U32 = mybir.dt.uint32
+U8 = mybir.dt.uint8
+E4M3 = mybir.dt.float8_e4m3fn_x4
+E5M2 = mybir.dt.float8_e5m2_x4
+COPY = mybir.ActivationFunctionType.Copy
+MULT = mybir.AluOpType.mult
+ADD = mybir.AluOpType.add
+
+FLOPS = 2 * M * N * R * 2
+
+P = 128
+KG = M // 512
+NC = N // 512
+UNITS = M // 256
+
+def tile_right_factor_refresh_e3_kernel(tc, g_words, g_scales, left, right_prev, gain, h, right_out, sketch_out):
+    nc = tc.nc
+    with ExitStack() as ctx:
+        keep = ctx.enter_context(tc.tile_pool(name="keep", bufs=1))
+        work = ctx.enter_context(tc.tile_pool(name="work", bufs=2))
+        psum_a = ctx.enter_context(tc.psum_pool(name="psum_a", bufs=4))
+        psum_b = ctx.enter_context(tc.psum_pool(name="psum_b", bufs=4))
+        ctx.enter_context(tc.manual_schedule())
+
+        gw = g_words.rearrange("g p n t -> p g (n t)")
+        gs = g_scales.rearrange("g (q r) n -> r q g n", r=4)
+        gs_raw = keep.tile([P, KG, N], U8, name="gs_raw", align_bytes=64)
+        nc.vector.memset(gs_raw[:].rearrange("p g n -> p (g n)").bitcast(I32), 0)
+        ident = keep.tile([P, P], F32, name="ident", align_bytes=64)
+        make_identity(nc, ident[:])
+        l_raw, g_raw, h_raw, rp = [], [], [], {}
+
+        def load_left(g):
+            t = work.tile([P, 4, 512], BF16, name="b4", tag="b4", bufs=4, align_bytes=64)
+            nc.sync.dma_start(out=t[:], in_=left[512 * g : 512 * (g + 1), :].rearrange("(p j) w -> p j w", j=4))
+            l_raw.append(t)
+
+        def load_scales():
+            for r in range(4):
+                nc.sync.dma_start(out=gs_raw[:].bitcast(I32)[r:P:32, :, :], in_=gs[r].bitcast(I32))
+
+        def load_g01(g, parts):
+            t = work.tile([P, 1024], I32, name="g_o", tag="g_o", bufs=4, align_bytes=64)
+            for a, b in parts:
+                nc.sync.dma_start(out=t[:, a:b], in_=gw[:, g, 4 * a : 4 * b].bitcast(I32))
+            g_raw.append(t)
+
+        g_raw2 = keep.tile([P, KG, 512], I32, name="g_raw2", align_bytes=64)
+
+        def load_g2():
+            nc.sync.dma_start(out=g_raw2[:], in_=gw[:, :, 4096:6144].bitcast(I32))
+
+        def load_rp(c):
+            t = keep.tile([P, 4, R], BF16, name=f"rp{c}", align_bytes=64)
+            nc.sync.dma_start(out=t[:], in_=right_prev[512 * c : 512 * (c + 1), :].rearrange("(p t) w -> p t w", t=4))
+            rp[c] = t
+
+        def load_h(u):
+            t = work.tile([P, 2, N], BF16, name="h_raw", tag="h_raw", bufs=6, align_bytes=64)
+            nc.sync.dma_start(out=t[:], in_=h[256 * u : 256 * (u + 1), :].rearrange("(p j) k -> p j k", j=2))
+            h_raw.append(t)
+
+        gain_b = keep.tile([P, NC, 4], BF16, name="gain_b", align_bytes=64)
+        nc.gpsimd.dma_start(out=gain_b[:], in_=gain.rearrange("(c p t) -> p c t", p=P, t=4))
+        gain_f = keep.tile([P, NC * 4], F32, name="gain_f", align_bytes=64)
+        nc.gpsimd.tensor_copy(out=gain_f[:], in_=gain_b[:].rearrange("p c t -> p (c t)"))
+        load_left(0)
+        load_scales()
+        load_g01(0, ((0, 512), (512, 1024)))
+        for g in range(1, KG):
+            load_left(g)
+            load_g01(g, ((0, 1024),))
+        load_g2()
+        load_rp(0)
+        load_rp(1)
+        load_h(0)
+        load_rp(2)
+        for u in range(1, 6):
+            load_h(u)
+
+        l_codes = keep.tile([P, KG, R], U32, name="l_codes", align_bytes=64)
+        l_scales = keep.tile([P, KG, R], U8, name="l_scales", align_bytes=64)
+        gs_perm = keep.tile([P, NC, 4, KG, P], U8, name="gs_perm", align_bytes=64)
+        g_perm = keep.tile([P, NC, 4, KG, P], I32, name="g_perm", align_bytes=64)
+        s_codes = keep.tile([P, NC, R], U32, name="s_codes", align_bytes=64)
+        s_scales = keep.tile([P, NC, R], U8, name="s_scales", align_bytes=64)
+        grp = {}
+
+        def perm_scales(c):
+            nc.vector.tensor_copy(out=gs_perm[:, c], in_=gs_raw[:, :, 512 * c : 512 * (c + 1)].rearrange("p g (q t) -> p t g q", t=4))
+
+        def perm_g(g, c):
+            nc.vector.tensor_copy(
+                out=g_perm[:, c, :, g, :].rearrange("p t (c i) -> p c t i", i=4),
+                in_=g_raw[g][:, 512 * c : 512 * (c + 1)].rearrange("p (c i t) -> p c t i", i=4, t=4))
+
+        def perm_g2():
+            nc.vector.tensor_copy(
+                out=g_perm[:, 2].rearrange("p t g q -> p t (g q)").rearrange("p t (c i) -> p c t i", i=4),
+                in_=g_raw2[:].rearrange("p g n -> p (g n)").rearrange("p (c i t) -> p c t i", i=4, t=4))
+
+        def interleave(copy, dst, src, a, b):
+            if a < b:
+                copy(out=dst[:, 4 * a : 4 * b].rearrange("p (c i j) -> p c j i", i=4, j=4),
+                     in_=src[:, :, a:b].rearrange("p j (c i) -> p c j i", i=4))
+
+        def left_copy(g, v):
+            t = work.tile([P, 4 * R], BF16, name="grp", tag="grp", bufs=3, align_bytes=64)
+            grp[g] = t
+            interleave(nc.vector.tensor_copy, t, l_raw[g], 0, v)
+            interleave(nc.scalar.copy, t, l_raw[g], v, R)
+
+        def left_quant(g):
+            nc.vector.quantize_mx(out=l_codes[:, g, :].bitcast(E4M3), scales=l_scales[:, g, :], in_=grp[g][:])
+
+        acc = {}
+
+        def s1_pass(c, t, g):
+            if g == 0:
+                acc[c, t] = (psum_b if c == 1 else psum_a).tile([P, R], F32, name="acc", tag="bank")
+            nc.tensor.matmul_mx(
+                out=acc[c, t][:],
+                lhsT=g_perm[:, c, t, g, :].bitcast(E5M2), lhsT_scale=gs_perm[:, c, t, g, :],
+                rhs=l_codes[:, g, :].bitcast(E4M3), rhs_scale=l_scales[:, g, :],
+                start=(g == 0), stop=(g == KG - 1))
+
+        right, scaled = {}, {}
+
+        def s1_out(c, t):
+            if t == 0:
+                right[c] = work.tile([P, 4, R], F32, name="right", tag="right", bufs=3, align_bytes=64)
+                scaled[c] = work.tile([P, 4, R], BF16, name="b4", tag="b4", bufs=4, align_bytes=64)
+            nc.vector.scalar_tensor_tensor(out=right[c][:, t, :], in0=rp[c][:, t, :], scalar=BETA, in1=acc[c, t][:], op0=MULT, op1=ADD)
+
+        def s1_act(c, t):
+            nc.gpsimd.tensor_scalar(out=scaled[c][:, t, :], in0=right[c][:, t, :], scalar1=gain_f[:, 4 * c + t : 4 * c + t + 1], scalar2=0.0, op0=MULT, op1=ADD)
+
+        def s1_store(c):
+            dst = right_out[512 * c : 512 * (c + 1), :].rearrange("(p t) w -> p t w", t=4)
+            nc.sync.dma_start(out=dst[:, 0:2, :], in_=right[c][:, 0:2, :])
+            nc.sync.dma_start(out=dst[:, 2:4, :], in_=right[c][:, 2:4, :])
+
+        sgrp = {}
+
+        def scaled_copy(c, v):
+            sgrp[c] = work.tile([P, 4 * R], BF16, name="grp", tag="grp", bufs=3, align_bytes=64)
+            interleave(nc.vector.tensor_copy, sgrp[c], scaled[c], 0, v)
+            interleave(nc.scalar.copy, sgrp[c], scaled[c], v, R)
+
+        def scaled_quant(c):
+            nc.vector.quantize_mx(out=s_codes[:, c, :].bitcast(E5M2), scales=s_scales[:, c, :], in_=sgrp[c][:])
+
+        banks, h_grp, h_codes, h_scales, h_words = {}, {}, {}, {}, {}
+
+        def h_sort(u):
+            h_words[u] = work.tile([P, 2 * NC, 2, P], F32, name="h_sorted", tag="h_sorted", bufs=2, align_bytes=64)
+            src = h_raw[u][:].rearrange("p j k -> p (j k)").bitcast(F32)
+            nc.vector.tensor_copy(out=h_words[u][:], in_=src.rearrange("p (b q w) -> p b w q", q=P, w=2))
+
+        def h_turn(u):
+            raw = h_raw[u][:].rearrange("p j k -> p (j k)").bitcast(F32)
+            for g in range(NC):
+                b = psum_b.tile([P, R], F32, name="turned", tag="bank")
+                banks[u, g] = b
+                for j in range(2):
+                    for w in range(2):
+                        lo = 768 * j + 256 * g + w
+                        src = h_words[u][:, 3 * j + g, w, :] if u in h_words else raw[:, lo : lo + 255 : 2]
+                        nc.tensor.transpose(b[:, P * (2 * j + w) : P * (2 * j + w + 1)], src, ident[:])
+
+        def h_copy(u, on_vector=()):
+            h_grp[u] = work.tile([P, NC, 1024], BF16, name="h_grp", tag="h_grp", bufs=3, align_bytes=64)
+            for g in range(NC):
+                (nc.vector.tensor_copy if g in on_vector else nc.scalar.copy)(
+                    out=h_grp[u][:, g, :].bitcast(F32).rearrange("p (j r w) -> p j r w", j=2, w=2),
+                    in_=banks[u, g][:].rearrange("p (j w r) -> p j r w", j=2, w=2))
+
+        def h_quant(u):
+            h_codes[u] = work.tile([P, NC, 256], U32, name="h_codes", tag="h_codes", bufs=5, align_bytes=64)
+            h_scales[u] = work.tile([P, NC, 256], U8, name="h_scales", tag="h_scales", bufs=5, align_bytes=64)
+            for g in range(NC):
+                nc.vector.quantize_mx(out=h_codes[u][:, g, :].bitcast(E4M3), scales=h_scales[u][:, g, :], in_=h_grp[u][:, g, :])
+
+        s2 = {}
+
+        def s2_mm(u, cs):
+            for j in range(2):
+                if cs[0] == 0:
+                    s2[u, j] = psum_a.tile([P, R], F32, name="acc", tag="bank")
+                for c in cs:
+                    nc.tensor.matmul_mx(
+                        out=s2[u, j][:],
+                        lhsT=h_codes[u][:, c, P * j : P * (j + 1)].bitcast(E4M3), lhsT_scale=h_scales[u][:, c, P * j : P * (j + 1)],
+                        rhs=s_codes[:, c, :].bitcast(E5M2), rhs_scale=s_scales[:, c, :],
+                        start=(c == 0), stop=(c == NC - 1))
+
+        out = {}
+
+        def s2_out(u, j, copy):
+            if j == 0:
+                out[u] = work.tile([P, 2, R], F32, name="g_o", tag="g_o", bufs=4, align_bytes=64)
+            copy(out=out[u][:, j, :], in_=s2[u, j][:])
+
+        def s2_store(u, split=False):
+            dst = sketch_out[256 * u : 256 * (u + 1), :].rearrange("(p j) w -> p j w", j=2)
+            if split:
+                for j in range(2):
+                    nc.sync.dma_start(out=dst[:, j, :], in_=out[u][:, j, :])
+            else:
+                nc.sync.dma_start(out=dst, in_=out[u][:])
+
+        V, S = nc.vector.tensor_copy, nc.scalar.copy
+        perm_scales(0)
+        for g in range(KG):
+            left_copy(g, 320 if g == 0 else 128)
+            perm_g(g, 0)
+            left_quant(g)
+            if g == 0:
+                perm_scales(1)
+            perm_g(g, 1)
+            for c in range(2):
+                for t in range(4):
+                    s1_pass(c, t, g)
+            if g == 2:
+                perm_scales(2)
+        perm_g2()
+        for t in range(4):
+            s1_out(0, t)
+            s1_act(0, t)
+        for t in range(4):
+            for g in range(KG):
+                s1_pass(2, t, g)
+        s1_out(1, 0)
+        s1_act(1, 0)
+        s1_out(1, 1)
+        s1_act(1, 1)
+        scaled_copy(0, 256)
+        s1_out(1, 2)
+        s1_act(1, 2)
+        s1_out(1, 3)
+        s1_act(1, 3)
+        scaled_quant(0)
+        s1_store(0)
+        h_turn(0)
+        s1_out(2, 0)
+        s1_act(2, 0)
+        s1_out(2, 1)
+        s1_act(2, 1)
+        h_copy(0)
+        scaled_copy(1, 256)
+        s1_out(2, 2)
+        s1_act(2, 2)
+        s1_out(2, 3)
+        s1_act(2, 3)
+        scaled_quant(1)
+        s1_store(1)
+        load_h(6)
+        h_turn(1)
+        h_quant(0)
+        h_copy(1)
+        scaled_copy(2, 384)
+        s1_store(2)
+        load_h(7)
+        scaled_quant(2)
+        h_turn(2)
+        h_sort(3)
+        h_quant(1)
+        h_copy(2)
+        s2_mm(0, (0, 1, 2))
+        h_turn(3)
+        h_quant(2)
+        s2_out(0, 0, V)
+        s2_out(0, 1, S)
+        s2_store(0)
+        h_copy(3)
+        h_sort(4)
+        h_quant(3)
+        for u in range(1, UNITS):
+            s2_mm(u, (0, 1, 2))
+            if u + 3 < UNITS:
+                h_turn(u + 3)
+                h_copy(u + 3)
+            s2_out(u, 0, V)
+            s2_out(u, 1, S)
+            s2_store(u, u == UNITS - 1)
+            if u + 4 < UNITS:
+                h_sort(u + 4)
+            if u + 3 < UNITS:
+                h_quant(u + 3)

@@ -5,6 +5,22 @@ from concourse.masks import make_identity
 
 M, N, R = 2048, 1536, 512
 BETA = 0.5
+FLOPS = 2 * (2 * M * N * R)
+
+P = 128
+GROUP = 512
+PACK = 4
+M_GROUPS = M // GROUP
+N_GROUPS = N // GROUP
+FIRST = 1024
+UNIT = 256
+UNITS = M // UNIT
+RAW_UNITS = 6
+
+LEFT_SHARE = (320, 384, 64, 128)
+SCALED_SHARE = (448, 448, 320)
+FIRST_SORTED_UNIT = 2
+FIRST_SHARED_UNIT = 6
 
 F32 = mybir.dt.float32
 BF16 = mybir.dt.bfloat16
@@ -13,288 +29,312 @@ U32 = mybir.dt.uint32
 U8 = mybir.dt.uint8
 E4M3 = mybir.dt.float8_e4m3fn_x4
 E5M2 = mybir.dt.float8_e5m2_x4
-COPY = mybir.ActivationFunctionType.Copy
-MULT = mybir.AluOpType.mult
-ADD = mybir.AluOpType.add
 
-FLOPS = 2 * M * N * R * 2
 
-P = 128
-KG = M // 512
-NC = N // 512
-UNITS = M // 256
+def interleave(nc, out, in_, share):
+    for copy, a, b in ((nc.vector.tensor_copy, 0, share), (nc.scalar.copy, share, R)):
+        copy(
+            out=out[:, PACK * a : PACK * b].rearrange("p (c i j) -> p c j i", i=4, j=PACK),
+            in_=in_[:, :, a:b].rearrange("p j (c i) -> p c j i", i=4),
+        )
 
-def tile_right_factor_refresh_e3_kernel(tc, g_words, g_scales, left, right_prev, gain, h, right_out, sketch_out):
+
+def tile_right_factor_refresh_e3_kernel(
+    tc, g_words, g_scales, left, right_prev, gain, h, right_out, sketch_out
+):
     nc = tc.nc
     with ExitStack() as ctx:
         keep = ctx.enter_context(tc.tile_pool(name="keep", bufs=1))
         work = ctx.enter_context(tc.tile_pool(name="work", bufs=2))
-        psum_a = ctx.enter_context(tc.psum_pool(name="psum_a", bufs=4))
-        psum_b = ctx.enter_context(tc.psum_pool(name="psum_b", bufs=4))
+        banks_a = ctx.enter_context(tc.psum_pool(name="banks_a", bufs=4))
+        banks_b = ctx.enter_context(tc.psum_pool(name="banks_b", bufs=4))
         ctx.enter_context(tc.manual_schedule())
 
-        gw = g_words.rearrange("g p n t -> p g (n t)")
-        gs = g_scales.rearrange("g (q r) n -> r q g n", r=4)
-        gs_raw = keep.tile([P, KG, N], U8, name="gs_raw", align_bytes=64)
-        nc.vector.memset(gs_raw[:].rearrange("p g n -> p (g n)").bitcast(I32), 0)
-        ident = keep.tile([P, P], F32, name="ident", align_bytes=64)
-        make_identity(nc, ident[:])
-        l_raw, g_raw, h_raw, rp = [], [], [], {}
+        scales_raw = keep.tile([P, M_GROUPS, N], U8, name="scales_raw", align_bytes=64)
+        nc.vector.memset(scales_raw[:].rearrange("p g n -> p (g n)").bitcast(I32), 0)
+
+        gain_raw = keep.tile([P, N_GROUPS, PACK], BF16, name="gain_raw", align_bytes=64)
+        nc.gpsimd.dma_start(out=gain_raw[:], in_=gain.rearrange("(c p t) -> p c t", p=P, t=PACK))
+        identity = keep.tile([P, P], F32, name="identity", align_bytes=64)
+        make_identity(nc, identity[:])
+        gain_col = keep.tile([P, N_GROUPS * PACK], F32, name="gain_col", align_bytes=64)
+        nc.gpsimd.tensor_copy(out=gain_col[:], in_=gain_raw[:].rearrange("p c t -> p (c t)"))
+
+        words_hbm = g_words.rearrange("g p n t -> p g (n t)")
+        left_raw, g_raw, prev, h_raw = [], [], [], []
 
         def load_left(g):
-            t = work.tile([P, 4, 512], BF16, name="b4", tag="b4", bufs=4, align_bytes=64)
-            nc.sync.dma_start(out=t[:], in_=left[512 * g : 512 * (g + 1), :].rearrange("(p j) w -> p j w", j=4))
-            l_raw.append(t)
+            rows = work.tile([P, PACK, R], BF16, name="rows", tag="rows", bufs=4, align_bytes=64)
+            nc.sync.dma_start(
+                out=rows[:], in_=left[GROUP * g : GROUP * (g + 1), :].rearrange("(p j) w -> p j w", j=PACK)
+            )
+            left_raw.append(rows)
 
         def load_scales():
+            rows_hbm = g_scales.rearrange("g (q r) n -> r q g n", r=4)
             for r in range(4):
-                nc.sync.dma_start(out=gs_raw[:].bitcast(I32)[r:P:32, :, :], in_=gs[r].bitcast(I32))
+                nc.sync.dma_start(out=scales_raw[:].bitcast(I32)[r:P:32, :, :], in_=rows_hbm[r].bitcast(I32))
 
-        def load_g01(g, parts):
-            t = work.tile([P, 1024], I32, name="g_o", tag="g_o", bufs=4, align_bytes=64)
-            for a, b in parts:
-                nc.sync.dma_start(out=t[:, a:b], in_=gw[:, g, 4 * a : 4 * b].bitcast(I32))
-            g_raw.append(t)
+        def load_g_first(g):
+            words = work.tile([P, FIRST], I32, name="four_kib", tag="four_kib", bufs=4, align_bytes=64)
+            nc.sync.dma_start(out=words[:], in_=words_hbm[:, g, 0 : 4 * FIRST].bitcast(I32))
+            g_raw.append(words)
 
-        g_raw2 = keep.tile([P, KG, 512], I32, name="g_raw2", align_bytes=64)
-
-        def load_g2():
-            nc.sync.dma_start(out=g_raw2[:], in_=gw[:, :, 4096:6144].bitcast(I32))
-
-        def load_rp(c):
-            t = keep.tile([P, 4, R], BF16, name=f"rp{c}", align_bytes=64)
-            nc.sync.dma_start(out=t[:], in_=right_prev[512 * c : 512 * (c + 1), :].rearrange("(p t) w -> p t w", t=4))
-            rp[c] = t
+        def load_prev(c):
+            rows = keep.tile([P, PACK, R], BF16, name=f"prev{c}", align_bytes=64)
+            nc.sync.dma_start(
+                out=rows[:], in_=right_prev[GROUP * c : GROUP * (c + 1), :].rearrange("(p t) w -> p t w", t=PACK)
+            )
+            prev.append(rows)
 
         def load_h(u):
-            t = work.tile([P, 2, N], BF16, name="h_raw", tag="h_raw", bufs=6, align_bytes=64)
-            nc.sync.dma_start(out=t[:], in_=h[256 * u : 256 * (u + 1), :].rearrange("(p j) k -> p j k", j=2))
-            h_raw.append(t)
+            rows = work.tile([P, 2, N], BF16, name="h_raw", tag="h_raw", bufs=RAW_UNITS, align_bytes=64)
+            nc.sync.dma_start(out=rows[:], in_=h[UNIT * u : UNIT * (u + 1), :].rearrange("(p j) k -> p j k", j=2))
+            h_raw.append(rows)
 
-        gain_b = keep.tile([P, NC, 4], BF16, name="gain_b", align_bytes=64)
-        nc.gpsimd.dma_start(out=gain_b[:], in_=gain.rearrange("(c p t) -> p c t", p=P, t=4))
-        gain_f = keep.tile([P, NC * 4], F32, name="gain_f", align_bytes=64)
-        nc.gpsimd.tensor_copy(out=gain_f[:], in_=gain_b[:].rearrange("p c t -> p (c t)"))
         load_left(0)
         load_scales()
-        load_g01(0, ((0, 512), (512, 1024)))
-        for g in range(1, KG):
+        load_g_first(0)
+        for g in range(1, M_GROUPS):
             load_left(g)
-            load_g01(g, ((0, 1024),))
-        load_g2()
-        load_rp(0)
-        load_rp(1)
-        load_h(0)
-        load_rp(2)
-        for u in range(1, 6):
+            load_g_first(g)
+        g_raw_rest = keep.tile([P, M_GROUPS, N - FIRST], I32, name="g_raw_rest", align_bytes=64)
+        nc.sync.dma_start(out=g_raw_rest[:], in_=words_hbm[:, :, 4 * FIRST :].bitcast(I32))
+        for c in range(N_GROUPS):
+            load_prev(c)
+        for u in range(RAW_UNITS):
             load_h(u)
 
-        l_codes = keep.tile([P, KG, R], U32, name="l_codes", align_bytes=64)
-        l_scales = keep.tile([P, KG, R], U8, name="l_scales", align_bytes=64)
-        gs_perm = keep.tile([P, NC, 4, KG, P], U8, name="gs_perm", align_bytes=64)
-        g_perm = keep.tile([P, NC, 4, KG, P], I32, name="g_perm", align_bytes=64)
-        s_codes = keep.tile([P, NC, R], U32, name="s_codes", align_bytes=64)
-        s_scales = keep.tile([P, NC, R], U8, name="s_scales", align_bytes=64)
-        grp = {}
+        widths = (FIRST // PACK, (N - FIRST) // PACK)
+        g_codes = [keep.tile([P, PACK, M_GROUPS, w], I32, name=f"g_codes{w}", align_bytes=64) for w in widths]
+        g_scale = [keep.tile([P, PACK, M_GROUPS, w], U8, name=f"g_scale{w}", align_bytes=64) for w in widths]
+        left_codes = keep.tile([P, M_GROUPS, R], U32, name="left_codes", align_bytes=64)
+        left_scale = keep.tile([P, M_GROUPS, R], U8, name="left_scale", align_bytes=64)
+        scaled_codes = keep.tile([P, N_GROUPS, R], U32, name="scaled_codes", align_bytes=64)
+        scaled_scale = keep.tile([P, N_GROUPS, R], U8, name="scaled_scale", align_bytes=64)
+        left_words, scaled_words = {}, {}
+        sums, right, scaled = {}, {}, {}
 
-        def perm_scales(c):
-            nc.vector.tensor_copy(out=gs_perm[:, c], in_=gs_raw[:, :, 512 * c : 512 * (c + 1)].rearrange("p g (q t) -> p t g q", t=4))
-
-        def perm_g(g, c):
+        def order_scales(part, g0, g1):
+            a, b = ((0, FIRST), (FIRST, N))[part]
             nc.vector.tensor_copy(
-                out=g_perm[:, c, :, g, :].rearrange("p t (c i) -> p c t i", i=4),
-                in_=g_raw[g][:, 512 * c : 512 * (c + 1)].rearrange("p (c i t) -> p c t i", i=4, t=4))
+                out=g_scale[part][:, :, g0:g1, :],
+                in_=scales_raw[:, g0:g1, a:b].rearrange("p g (q t) -> p t g q", t=PACK),
+            )
 
-        def perm_g2():
+        def order_words(out, in_):
             nc.vector.tensor_copy(
-                out=g_perm[:, 2].rearrange("p t g q -> p t (g q)").rearrange("p t (c i) -> p c t i", i=4),
-                in_=g_raw2[:].rearrange("p g n -> p (g n)").rearrange("p (c i t) -> p c t i", i=4, t=4))
+                out=out.rearrange("p t (c i) -> p c t i", i=4),
+                in_=in_.rearrange("p (c i t) -> p c t i", i=4, t=PACK),
+            )
 
-        def interleave(copy, dst, src, a, b):
-            if a < b:
-                copy(out=dst[:, 4 * a : 4 * b].rearrange("p (c i j) -> p c j i", i=4, j=4),
-                     in_=src[:, :, a:b].rearrange("p j (c i) -> p c j i", i=4))
+        def copy_left(g):
+            left_words[g] = work.tile([P, PACK * R], BF16, name="words", tag="words", bufs=3, align_bytes=64)
+            interleave(nc, left_words[g], left_raw[g], LEFT_SHARE[g])
 
-        def left_copy(g, v):
-            t = work.tile([P, 4 * R], BF16, name="grp", tag="grp", bufs=3, align_bytes=64)
-            grp[g] = t
-            interleave(nc.vector.tensor_copy, t, l_raw[g], 0, v)
-            interleave(nc.scalar.copy, t, l_raw[g], v, R)
+        def quantize_left(g):
+            nc.vector.quantize_mx(
+                out=left_codes[:, g, :].bitcast(E4M3), scales=left_scale[:, g, :], in_=left_words[g][:]
+            )
 
-        def left_quant(g):
-            nc.vector.quantize_mx(out=l_codes[:, g, :].bitcast(E4M3), scales=l_scales[:, g, :], in_=grp[g][:])
-
-        acc = {}
-
-        def s1_pass(c, t, g):
+        def multiply_g(c, t, g):
             if g == 0:
-                acc[c, t] = (psum_b if c == 1 else psum_a).tile([P, R], F32, name="acc", tag="bank")
+                sums[c, t] = (banks_b if c == 1 else banks_a).tile([P, R], F32, name="sums", tag="bank")
+            part, c_in_part = divmod(c, FIRST // GROUP)
+            q = slice(P * c_in_part, P * (c_in_part + 1))
             nc.tensor.matmul_mx(
-                out=acc[c, t][:],
-                lhsT=g_perm[:, c, t, g, :].bitcast(E5M2), lhsT_scale=gs_perm[:, c, t, g, :],
-                rhs=l_codes[:, g, :].bitcast(E4M3), rhs_scale=l_scales[:, g, :],
-                start=(g == 0), stop=(g == KG - 1))
+                out=sums[c, t][:],
+                lhsT=g_codes[part][:, t, g, q].bitcast(E5M2),
+                lhsT_scale=g_scale[part][:, t, g, q],
+                rhs=left_codes[:, g, :].bitcast(E4M3),
+                rhs_scale=left_scale[:, g, :],
+                start=(g == 0),
+                stop=(g == M_GROUPS - 1),
+            )
 
-        right, scaled = {}, {}
+        def finish_right(c, k):
+            if k == 0:
+                right[c] = work.tile([P, PACK, R], F32, name="right", tag="right", bufs=3, align_bytes=64)
+                scaled[c] = work.tile([P, PACK, R], BF16, name="rows", tag="rows", bufs=4, align_bytes=64)
+            for t in (2 * k, 2 * k + 1):
+                nc.vector.scalar_tensor_tensor(
+                    out=right[c][:, t, :],
+                    in0=prev[c][:, t, :],
+                    scalar=BETA,
+                    in1=sums[c, t][:],
+                    op0=mybir.AluOpType.mult,
+                    op1=mybir.AluOpType.add,
+                )
+                nc.scalar.activation(
+                    out=scaled[c][:, t, :],
+                    in_=right[c][:, t, :],
+                    func=mybir.ActivationFunctionType.Copy,
+                    scale=gain_col[:, PACK * c + t : PACK * c + t + 1],
+                )
 
-        def s1_out(c, t):
-            if t == 0:
-                right[c] = work.tile([P, 4, R], F32, name="right", tag="right", bufs=3, align_bytes=64)
-                scaled[c] = work.tile([P, 4, R], BF16, name="b4", tag="b4", bufs=4, align_bytes=64)
-            nc.vector.scalar_tensor_tensor(out=right[c][:, t, :], in0=rp[c][:, t, :], scalar=BETA, in1=acc[c, t][:], op0=MULT, op1=ADD)
+        def store_right(c, k):
+            rows = right_out[GROUP * c : GROUP * (c + 1), :].rearrange("(p t) w -> p t w", t=PACK)
+            nc.sync.dma_start(out=rows[:, 2 * k : 2 * k + 2, :], in_=right[c][:, 2 * k : 2 * k + 2, :])
 
-        def s1_act(c, t):
-            nc.gpsimd.tensor_scalar(out=scaled[c][:, t, :], in0=right[c][:, t, :], scalar1=gain_f[:, 4 * c + t : 4 * c + t + 1], scalar2=0.0, op0=MULT, op1=ADD)
+        def copy_scaled(c):
+            scaled_words[c] = work.tile([P, PACK * R], BF16, name="words", tag="words", bufs=3, align_bytes=64)
+            interleave(nc, scaled_words[c], scaled[c], SCALED_SHARE[c])
 
-        def s1_store(c):
-            dst = right_out[512 * c : 512 * (c + 1), :].rearrange("(p t) w -> p t w", t=4)
-            nc.sync.dma_start(out=dst[:, 0:2, :], in_=right[c][:, 0:2, :])
-            nc.sync.dma_start(out=dst[:, 2:4, :], in_=right[c][:, 2:4, :])
+        def quantize_scaled(c):
+            nc.vector.quantize_mx(
+                out=scaled_codes[:, c, :].bitcast(E5M2), scales=scaled_scale[:, c, :], in_=scaled_words[c][:]
+            )
 
-        sgrp = {}
+        h_sorted, turned, h_words, h_codes, h_scale = {}, {}, {}, {}, {}
+        products, sketch = {}, {}
 
-        def scaled_copy(c, v):
-            sgrp[c] = work.tile([P, 4 * R], BF16, name="grp", tag="grp", bufs=3, align_bytes=64)
-            interleave(nc.vector.tensor_copy, sgrp[c], scaled[c], 0, v)
-            interleave(nc.scalar.copy, sgrp[c], scaled[c], v, R)
+        def sort_h(u):
+            h_sorted[u] = work.tile([P, 2 * N_GROUPS, 2, P], F32, name="h_sorted", tag="h_sorted", align_bytes=64)
+            words = h_raw[u][:].rearrange("p j k -> p (j k)").bitcast(F32)
+            nc.vector.tensor_copy(out=h_sorted[u][:], in_=words.rearrange("p (b q w) -> p b w q", q=P, w=2))
 
-        def scaled_quant(c):
-            nc.vector.quantize_mx(out=s_codes[:, c, :].bitcast(E5M2), scales=s_scales[:, c, :], in_=sgrp[c][:])
-
-        banks, h_grp, h_codes, h_scales, h_words = {}, {}, {}, {}, {}
-
-        def h_sort(u):
-            h_words[u] = work.tile([P, 2 * NC, 2, P], F32, name="h_sorted", tag="h_sorted", bufs=2, align_bytes=64)
-            src = h_raw[u][:].rearrange("p j k -> p (j k)").bitcast(F32)
-            nc.vector.tensor_copy(out=h_words[u][:], in_=src.rearrange("p (b q w) -> p b w q", q=P, w=2))
-
-        def h_turn(u):
+        def turn_h(u):
             raw = h_raw[u][:].rearrange("p j k -> p (j k)").bitcast(F32)
-            for g in range(NC):
-                b = psum_b.tile([P, R], F32, name="turned", tag="bank")
-                banks[u, g] = b
+            for g in range(N_GROUPS):
+                turned[u, g] = banks_b.tile([P, R], F32, name="turned", tag="bank")
                 for j in range(2):
                     for w in range(2):
-                        lo = 768 * j + 256 * g + w
-                        src = h_words[u][:, 3 * j + g, w, :] if u in h_words else raw[:, lo : lo + 255 : 2]
-                        nc.tensor.transpose(b[:, P * (2 * j + w) : P * (2 * j + w + 1)], src, ident[:])
+                        if u < FIRST_SORTED_UNIT:
+                            x = (N * j + GROUP * g) // 2 + w
+                            words = raw[:, x : x + 2 * P - 1 : 2]
+                        else:
+                            words = h_sorted[u][:, N_GROUPS * j + g, w, :]
+                        z = P * (2 * j + w)
+                        nc.tensor.transpose(turned[u, g][:, z : z + P], words, identity[:])
 
-        def h_copy(u, on_vector=()):
-            h_grp[u] = work.tile([P, NC, 1024], BF16, name="h_grp", tag="h_grp", bufs=3, align_bytes=64)
-            for g in range(NC):
-                (nc.vector.tensor_copy if g in on_vector else nc.scalar.copy)(
-                    out=h_grp[u][:, g, :].bitcast(F32).rearrange("p (j r w) -> p j r w", j=2, w=2),
-                    in_=banks[u, g][:].rearrange("p (j w r) -> p j r w", j=2, w=2))
+        def copy_h(u):
+            h_words[u] = work.tile([P, N_GROUPS, PACK * UNIT], BF16, name="h_words", tag="h_words", bufs=3, align_bytes=64)
+            for g in range(N_GROUPS):
+                on_vector = u >= FIRST_SHARED_UNIT and g == N_GROUPS - 1
+                (nc.vector.tensor_copy if on_vector else nc.scalar.copy)(
+                    out=h_words[u][:, g, :].bitcast(F32).rearrange("p (j r w) -> p j r w", j=2, w=2),
+                    in_=turned[u, g][:].rearrange("p (j w r) -> p j r w", j=2, w=2),
+                )
 
-        def h_quant(u):
-            h_codes[u] = work.tile([P, NC, 256], U32, name="h_codes", tag="h_codes", bufs=5, align_bytes=64)
-            h_scales[u] = work.tile([P, NC, 256], U8, name="h_scales", tag="h_scales", bufs=5, align_bytes=64)
-            for g in range(NC):
-                nc.vector.quantize_mx(out=h_codes[u][:, g, :].bitcast(E4M3), scales=h_scales[u][:, g, :], in_=h_grp[u][:, g, :])
+        def quantize_h(u):
+            h_codes[u] = work.tile([P, N_GROUPS, UNIT], U32, name="h_codes", tag="h_codes", bufs=5, align_bytes=64)
+            h_scale[u] = work.tile([P, N_GROUPS, UNIT], U8, name="h_scale", tag="h_scale", bufs=5, align_bytes=64)
+            for groups in (slice(0, 2), slice(2, 3)):
+                nc.vector.quantize_mx(
+                    out=h_codes[u][:, groups, :].rearrange("p g m -> p (g m)").bitcast(E4M3),
+                    scales=h_scale[u][:, groups, :].rearrange("p g m -> p (g m)"),
+                    in_=h_words[u][:, groups, :].rearrange("p g x -> p (g x)"),
+                )
 
-        s2 = {}
-
-        def s2_mm(u, cs):
+        def multiply_h(u, groups=range(N_GROUPS)):
             for j in range(2):
-                if cs[0] == 0:
-                    s2[u, j] = psum_a.tile([P, R], F32, name="acc", tag="bank")
-                for c in cs:
+                if groups[0] == 0:
+                    products[u, j] = banks_a.tile([P, R], F32, name="products", tag="bank")
+                rows = slice(P * j, P * (j + 1))
+                for c in groups:
                     nc.tensor.matmul_mx(
-                        out=s2[u, j][:],
-                        lhsT=h_codes[u][:, c, P * j : P * (j + 1)].bitcast(E4M3), lhsT_scale=h_scales[u][:, c, P * j : P * (j + 1)],
-                        rhs=s_codes[:, c, :].bitcast(E5M2), rhs_scale=s_scales[:, c, :],
-                        start=(c == 0), stop=(c == NC - 1))
+                        out=products[u, j][:],
+                        lhsT=h_codes[u][:, c, rows].bitcast(E4M3),
+                        lhsT_scale=h_scale[u][:, c, rows],
+                        rhs=scaled_codes[:, c, :].bitcast(E5M2),
+                        rhs_scale=scaled_scale[:, c, :],
+                        start=(c == 0),
+                        stop=(c == N_GROUPS - 1),
+                    )
 
-        out = {}
-
-        def s2_out(u, j, copy):
-            if j == 0:
-                out[u] = work.tile([P, 2, R], F32, name="g_o", tag="g_o", bufs=4, align_bytes=64)
-            copy(out=out[u][:, j, :], in_=s2[u, j][:])
-
-        def s2_store(u, split=False):
-            dst = sketch_out[256 * u : 256 * (u + 1), :].rearrange("(p j) w -> p j w", j=2)
-            if split:
-                for j in range(2):
-                    nc.sync.dma_start(out=dst[:, j, :], in_=out[u][:, j, :])
+        def store_sketch(u):
+            sketch[u] = work.tile([P, 2, R], F32, name="four_kib", tag="four_kib", bufs=4, align_bytes=64)
+            rows = sketch_out[UNIT * u : UNIT * (u + 1), :].rearrange("(p j) w -> p j w", j=2)
+            copy_first = nc.vector.tensor_copy if u >= FIRST_SHARED_UNIT else nc.scalar.copy
+            copy_first(out=sketch[u][:, 0, :], in_=products[u, 0][:])
+            if u < UNITS - 1:
+                nc.scalar.copy(out=sketch[u][:, 1, :], in_=products[u, 1][:])
+                nc.sync.dma_start(out=rows, in_=sketch[u][:])
             else:
-                nc.sync.dma_start(out=dst, in_=out[u][:])
+                half = R // 2
+                nc.vector.tensor_copy(out=sketch[u][:, 1, :half], in_=products[u, 1][:, :half])
+                nc.scalar.copy(out=sketch[u][:, 1, half:], in_=products[u, 1][:, half:])
+                nc.sync.dma_start(out=rows[:, 0, :], in_=sketch[u][:, 0, :])
+                nc.sync.dma_start(out=rows[:, 1, :half], in_=sketch[u][:, 1, :half])
+                nc.scalar.dma_start(out=rows[:, 1, half:], in_=sketch[u][:, 1, half:])
 
-        V, S = nc.vector.tensor_copy, nc.scalar.copy
-        perm_scales(0)
-        for g in range(KG):
-            left_copy(g, 320 if g == 0 else 128)
-            perm_g(g, 0)
-            left_quant(g)
+        for g in range(M_GROUPS):
+            copy_left(g)
             if g == 0:
-                perm_scales(1)
-            perm_g(g, 1)
-            for c in range(2):
-                for t in range(4):
-                    s1_pass(c, t, g)
+                quantize_left(g)
+                order_scales(0, 0, 1)
+                order_words(g_codes[0][:, :, g, :], g_raw[g][:])
+                order_scales(0, 1, M_GROUPS)
+            else:
+                order_words(g_codes[0][:, :, g, :], g_raw[g][:])
+                quantize_left(g)
+            for c in range(FIRST // GROUP):
+                for t in range(PACK):
+                    multiply_g(c, t, g)
             if g == 2:
-                perm_scales(2)
-        perm_g2()
-        for t in range(4):
-            s1_out(0, t)
-            s1_act(0, t)
-        for t in range(4):
-            for g in range(KG):
-                s1_pass(2, t, g)
-        s1_out(1, 0)
-        s1_act(1, 0)
-        s1_out(1, 1)
-        s1_act(1, 1)
-        scaled_copy(0, 256)
-        s1_out(1, 2)
-        s1_act(1, 2)
-        s1_out(1, 3)
-        s1_act(1, 3)
-        scaled_quant(0)
-        s1_store(0)
-        h_turn(0)
-        s1_out(2, 0)
-        s1_act(2, 0)
-        s1_out(2, 1)
-        s1_act(2, 1)
-        h_copy(0)
-        scaled_copy(1, 256)
-        s1_out(2, 2)
-        s1_act(2, 2)
-        s1_out(2, 3)
-        s1_act(2, 3)
-        scaled_quant(1)
-        s1_store(1)
+                order_scales(1, 0, M_GROUPS)
+
+        order_words(
+            g_codes[1][:].rearrange("p t g q -> p t (g q)"),
+            g_raw_rest[:].rearrange("p g n -> p (g n)"),
+        )
+        for k in range(2):
+            finish_right(0, k)
+            store_right(0, k)
+        for t in (0, 1):
+            for g in range(M_GROUPS):
+                multiply_g(2, t, g)
+        for k in range(2):
+            finish_right(1, k)
+            store_right(1, k)
+        copy_scaled(0)
+        turn_h(0)
+        copy_h(0)
         load_h(6)
-        h_turn(1)
-        h_quant(0)
-        h_copy(1)
-        scaled_copy(2, 384)
-        s1_store(2)
+        copy_scaled(1)
+        for t in (2, 3):
+            for g in range(M_GROUPS):
+                multiply_g(2, t, g)
+        turn_h(1)
         load_h(7)
-        scaled_quant(2)
-        h_turn(2)
-        h_sort(3)
-        h_quant(1)
-        h_copy(2)
-        s2_mm(0, (0, 1, 2))
-        h_turn(3)
-        h_quant(2)
-        s2_out(0, 0, V)
-        s2_out(0, 1, S)
-        s2_store(0)
-        h_copy(3)
-        h_sort(4)
-        h_quant(3)
-        for u in range(1, UNITS):
-            s2_mm(u, (0, 1, 2))
-            if u + 3 < UNITS:
-                h_turn(u + 3)
-                h_copy(u + 3)
-            s2_out(u, 0, V)
-            s2_out(u, 1, S)
-            s2_store(u, u == UNITS - 1)
-            if u + 4 < UNITS:
-                h_sort(u + 4)
-            if u + 3 < UNITS:
-                h_quant(u + 3)
+        for k in range(2):
+            finish_right(2, k)
+        for k in range(2):
+            store_right(2, k)
+        sort_h(2)
+        copy_h(1)
+        quantize_scaled(0)
+        turn_h(2)
+        copy_h(2)
+        sort_h(3)
+        quantize_scaled(1)
+        quantize_h(0)
+        sort_h(4)
+        copy_scaled(2)
+        turn_h(3)
+        multiply_h(0, (0, 1))
+        copy_h(3)
+        quantize_scaled(2)
+        quantize_h(1)
+        turn_h(4)
+        multiply_h(0, (2,))
+        quantize_h(2)
+        sort_h(5)
+        quantize_h(3)
+        store_sketch(0)
+        multiply_h(1)
+
+        for u in range(5, UNITS):
+            multiply_h(u - 3)
+            store_sketch(u - 4)
+            copy_h(u - 1)
+            quantize_h(u - 1)
+            turn_h(u)
+            if u + 1 < UNITS:
+                sort_h(u + 1)
+        copy_h(UNITS - 1)
+        quantize_h(UNITS - 1)
+        store_sketch(UNITS - 4)
+        for u in range(UNITS - 3, UNITS):
+            multiply_h(u)
+            store_sketch(u)

from contextlib import ExitStack

import concourse.mybir as mybir
from concourse.masks import make_identity

M, N, R = 2048, 1536, 512
BETA = 0.5
FLOPS = 2 * (2 * M * N * R)

P = 128
GROUP = 512
PACK = 4
M_GROUPS = M // GROUP
N_GROUPS = N // GROUP
FIRST = 1024
UNIT = 256
UNITS = M // UNIT
RAW_UNITS = 6

LEFT_SHARE = (320, 384, 64, 128)
SCALED_SHARE = (448, 448, 320)
FIRST_SORTED_UNIT = 2
FIRST_SHARED_UNIT = 6

F32 = mybir.dt.float32
BF16 = mybir.dt.bfloat16
I32 = mybir.dt.int32
U32 = mybir.dt.uint32
U8 = mybir.dt.uint8
E4M3 = mybir.dt.float8_e4m3fn_x4
E5M2 = mybir.dt.float8_e5m2_x4


def interleave(nc, out, in_, share):
    for copy, a, b in ((nc.vector.tensor_copy, 0, share), (nc.scalar.copy, share, R)):
        copy(
            out=out[:, PACK * a : PACK * b].rearrange("p (c i j) -> p c j i", i=4, j=PACK),
            in_=in_[:, :, a:b].rearrange("p j (c i) -> p c j i", i=4),
        )


def tile_right_factor_refresh_e3_kernel(
    tc, g_words, g_scales, left, right_prev, gain, h, right_out, sketch_out
):
    nc = tc.nc
    with ExitStack() as ctx:
        keep = ctx.enter_context(tc.tile_pool(name="keep", bufs=1))
        work = ctx.enter_context(tc.tile_pool(name="work", bufs=2))
        banks_a = ctx.enter_context(tc.psum_pool(name="banks_a", bufs=4))
        banks_b = ctx.enter_context(tc.psum_pool(name="banks_b", bufs=4))
        ctx.enter_context(tc.manual_schedule())

        scales_raw = keep.tile([P, M_GROUPS, N], U8, name="scales_raw", align_bytes=64)
        nc.vector.memset(scales_raw[:].rearrange("p g n -> p (g n)").bitcast(I32), 0)

        gain_raw = keep.tile([P, N_GROUPS, PACK], BF16, name="gain_raw", align_bytes=64)
        nc.gpsimd.dma_start(out=gain_raw[:], in_=gain.rearrange("(c p t) -> p c t", p=P, t=PACK))
        identity = keep.tile([P, P], F32, name="identity", align_bytes=64)
        make_identity(nc, identity[:])
        gain_col = keep.tile([P, N_GROUPS * PACK], F32, name="gain_col", align_bytes=64)
        nc.gpsimd.tensor_copy(out=gain_col[:], in_=gain_raw[:].rearrange("p c t -> p (c t)"))

        words_hbm = g_words.rearrange("g p n t -> p g (n t)")
        left_raw, g_raw, prev, h_raw = [], [], [], []

        def load_left(g):
            rows = work.tile([P, PACK, R], BF16, name="rows", tag="rows", bufs=4, align_bytes=64)
            nc.sync.dma_start(
                out=rows[:], in_=left[GROUP * g : GROUP * (g + 1), :].rearrange("(p j) w -> p j w", j=PACK)
            )
            left_raw.append(rows)

        def load_scales():
            rows_hbm = g_scales.rearrange("g (q r) n -> r q g n", r=4)
            for r in range(4):
                nc.sync.dma_start(out=scales_raw[:].bitcast(I32)[r:P:32, :, :], in_=rows_hbm[r].bitcast(I32))

        def load_g_first(g):
            words = work.tile([P, FIRST], I32, name="four_kib", tag="four_kib", bufs=4, align_bytes=64)
            nc.sync.dma_start(out=words[:], in_=words_hbm[:, g, 0 : 4 * FIRST].bitcast(I32))
            g_raw.append(words)

        def load_prev(c):
            rows = keep.tile([P, PACK, R], BF16, name=f"prev{c}", align_bytes=64)
            nc.sync.dma_start(
                out=rows[:], in_=right_prev[GROUP * c : GROUP * (c + 1), :].rearrange("(p t) w -> p t w", t=PACK)
            )
            prev.append(rows)

        def load_h(u):
            rows = work.tile([P, 2, N], BF16, name="h_raw", tag="h_raw", bufs=RAW_UNITS, align_bytes=64)
            nc.sync.dma_start(out=rows[:], in_=h[UNIT * u : UNIT * (u + 1), :].rearrange("(p j) k -> p j k", j=2))
            h_raw.append(rows)

        load_left(0)
        load_scales()
        load_g_first(0)
        for g in range(1, M_GROUPS):
            load_left(g)
            load_g_first(g)
        g_raw_rest = keep.tile([P, M_GROUPS, N - FIRST], I32, name="g_raw_rest", align_bytes=64)
        nc.sync.dma_start(out=g_raw_rest[:], in_=words_hbm[:, :, 4 * FIRST :].bitcast(I32))
        for c in range(N_GROUPS):
            load_prev(c)
        for u in range(RAW_UNITS):
            load_h(u)

        widths = (FIRST // PACK, (N - FIRST) // PACK)
        g_codes = [keep.tile([P, PACK, M_GROUPS, w], I32, name=f"g_codes{w}", align_bytes=64) for w in widths]
        g_scale = [keep.tile([P, PACK, M_GROUPS, w], U8, name=f"g_scale{w}", align_bytes=64) for w in widths]
        left_codes = keep.tile([P, M_GROUPS, R], U32, name="left_codes", align_bytes=64)
        left_scale = keep.tile([P, M_GROUPS, R], U8, name="left_scale", align_bytes=64)
        scaled_codes = keep.tile([P, N_GROUPS, R], U32, name="scaled_codes", align_bytes=64)
        scaled_scale = keep.tile([P, N_GROUPS, R], U8, name="scaled_scale", align_bytes=64)
        left_words, scaled_words = {}, {}
        sums, right, scaled = {}, {}, {}

        def order_scales(part, g0, g1):
            a, b = ((0, FIRST), (FIRST, N))[part]
            nc.vector.tensor_copy(
                out=g_scale[part][:, :, g0:g1, :],
                in_=scales_raw[:, g0:g1, a:b].rearrange("p g (q t) -> p t g q", t=PACK),
            )

        def order_words(out, in_):
            nc.vector.tensor_copy(
                out=out.rearrange("p t (c i) -> p c t i", i=4),
                in_=in_.rearrange("p (c i t) -> p c t i", i=4, t=PACK),
            )

        def copy_left(g):
            left_words[g] = work.tile([P, PACK * R], BF16, name="words", tag="words", bufs=3, align_bytes=64)
            interleave(nc, left_words[g], left_raw[g], LEFT_SHARE[g])

        def quantize_left(g):
            nc.vector.quantize_mx(
                out=left_codes[:, g, :].bitcast(E4M3), scales=left_scale[:, g, :], in_=left_words[g][:]
            )

        def multiply_g(c, t, g):
            if g == 0:
                sums[c, t] = (banks_b if c == 1 else banks_a).tile([P, R], F32, name="sums", tag="bank")
            part, c_in_part = divmod(c, FIRST // GROUP)
            q = slice(P * c_in_part, P * (c_in_part + 1))
            nc.tensor.matmul_mx(
                out=sums[c, t][:],
                lhsT=g_codes[part][:, t, g, q].bitcast(E5M2),
                lhsT_scale=g_scale[part][:, t, g, q],
                rhs=left_codes[:, g, :].bitcast(E4M3),
                rhs_scale=left_scale[:, g, :],
                start=(g == 0),
                stop=(g == M_GROUPS - 1),
            )

        def finish_right(c, k):
            if k == 0:
                right[c] = work.tile([P, PACK, R], F32, name="right", tag="right", bufs=3, align_bytes=64)
                scaled[c] = work.tile([P, PACK, R], BF16, name="rows", tag="rows", bufs=4, align_bytes=64)
            for t in (2 * k, 2 * k + 1):
                nc.vector.scalar_tensor_tensor(
                    out=right[c][:, t, :],
                    in0=prev[c][:, t, :],
                    scalar=BETA,
                    in1=sums[c, t][:],
                    op0=mybir.AluOpType.mult,
                    op1=mybir.AluOpType.add,
                )
                nc.scalar.activation(
                    out=scaled[c][:, t, :],
                    in_=right[c][:, t, :],
                    func=mybir.ActivationFunctionType.Copy,
                    scale=gain_col[:, PACK * c + t : PACK * c + t + 1],
                )

        def store_right(c, k):
            rows = right_out[GROUP * c : GROUP * (c + 1), :].rearrange("(p t) w -> p t w", t=PACK)
            nc.sync.dma_start(out=rows[:, 2 * k : 2 * k + 2, :], in_=right[c][:, 2 * k : 2 * k + 2, :])

        def copy_scaled(c):
            scaled_words[c] = work.tile([P, PACK * R], BF16, name="words", tag="words", bufs=3, align_bytes=64)
            interleave(nc, scaled_words[c], scaled[c], SCALED_SHARE[c])

        def quantize_scaled(c):
            nc.vector.quantize_mx(
                out=scaled_codes[:, c, :].bitcast(E5M2), scales=scaled_scale[:, c, :], in_=scaled_words[c][:]
            )

        h_sorted, turned, h_words, h_codes, h_scale = {}, {}, {}, {}, {}
        products, sketch = {}, {}

        def sort_h(u):
            h_sorted[u] = work.tile([P, 2 * N_GROUPS, 2, P], F32, name="h_sorted", tag="h_sorted", align_bytes=64)
            words = h_raw[u][:].rearrange("p j k -> p (j k)").bitcast(F32)
            nc.vector.tensor_copy(out=h_sorted[u][:], in_=words.rearrange("p (b q w) -> p b w q", q=P, w=2))

        def turn_h(u):
            raw = h_raw[u][:].rearrange("p j k -> p (j k)").bitcast(F32)
            for g in range(N_GROUPS):
                turned[u, g] = banks_b.tile([P, R], F32, name="turned", tag="bank")
                for j in range(2):
                    for w in range(2):
                        if u < FIRST_SORTED_UNIT:
                            x = (N * j + GROUP * g) // 2 + w
                            words = raw[:, x : x + 2 * P - 1 : 2]
                        else:
                            words = h_sorted[u][:, N_GROUPS * j + g, w, :]
                        z = P * (2 * j + w)
                        nc.tensor.transpose(turned[u, g][:, z : z + P], words, identity[:])

        def copy_h(u):
            h_words[u] = work.tile([P, N_GROUPS, PACK * UNIT], BF16, name="h_words", tag="h_words", bufs=3, align_bytes=64)
            for g in range(N_GROUPS):
                on_vector = u >= FIRST_SHARED_UNIT and g == N_GROUPS - 1
                (nc.vector.tensor_copy if on_vector else nc.scalar.copy)(
                    out=h_words[u][:, g, :].bitcast(F32).rearrange("p (j r w) -> p j r w", j=2, w=2),
                    in_=turned[u, g][:].rearrange("p (j w r) -> p j r w", j=2, w=2),
                )

        def quantize_h(u):
            h_codes[u] = work.tile([P, N_GROUPS, UNIT], U32, name="h_codes", tag="h_codes", bufs=5, align_bytes=64)
            h_scale[u] = work.tile([P, N_GROUPS, UNIT], U8, name="h_scale", tag="h_scale", bufs=5, align_bytes=64)
            for groups in (slice(0, 2), slice(2, 3)):
                nc.vector.quantize_mx(
                    out=h_codes[u][:, groups, :].rearrange("p g m -> p (g m)").bitcast(E4M3),
                    scales=h_scale[u][:, groups, :].rearrange("p g m -> p (g m)"),
                    in_=h_words[u][:, groups, :].rearrange("p g x -> p (g x)"),
                )

        def multiply_h(u, groups=range(N_GROUPS)):
            for j in range(2):
                if groups[0] == 0:
                    products[u, j] = banks_a.tile([P, R], F32, name="products", tag="bank")
                rows = slice(P * j, P * (j + 1))
                for c in groups:
                    nc.tensor.matmul_mx(
                        out=products[u, j][:],
                        lhsT=h_codes[u][:, c, rows].bitcast(E4M3),
                        lhsT_scale=h_scale[u][:, c, rows],
                        rhs=scaled_codes[:, c, :].bitcast(E5M2),
                        rhs_scale=scaled_scale[:, c, :],
                        start=(c == 0),
                        stop=(c == N_GROUPS - 1),
                    )

        def store_sketch(u):
            sketch[u] = work.tile([P, 2, R], F32, name="four_kib", tag="four_kib", bufs=4, align_bytes=64)
            rows = sketch_out[UNIT * u : UNIT * (u + 1), :].rearrange("(p j) w -> p j w", j=2)
            copy_first = nc.vector.tensor_copy if u >= FIRST_SHARED_UNIT else nc.scalar.copy
            copy_first(out=sketch[u][:, 0, :], in_=products[u, 0][:])
            if u < UNITS - 1:
                nc.scalar.copy(out=sketch[u][:, 1, :], in_=products[u, 1][:])
                nc.sync.dma_start(out=rows, in_=sketch[u][:])
            else:
                half = R // 2
                nc.vector.tensor_copy(out=sketch[u][:, 1, :half], in_=products[u, 1][:, :half])
                nc.scalar.copy(out=sketch[u][:, 1, half:], in_=products[u, 1][:, half:])
                nc.sync.dma_start(out=rows[:, 0, :], in_=sketch[u][:, 0, :])
                nc.sync.dma_start(out=rows[:, 1, :half], in_=sketch[u][:, 1, :half])
                nc.scalar.dma_start(out=rows[:, 1, half:], in_=sketch[u][:, 1, half:])

        for g in range(M_GROUPS):
            copy_left(g)
            if g == 0:
                quantize_left(g)
                order_scales(0, 0, 1)
                order_words(g_codes[0][:, :, g, :], g_raw[g][:])
                order_scales(0, 1, M_GROUPS)
            else:
                order_words(g_codes[0][:, :, g, :], g_raw[g][:])
                quantize_left(g)
            for c in range(FIRST // GROUP):
                for t in range(PACK):
                    multiply_g(c, t, g)
            if g == 2:
                order_scales(1, 0, M_GROUPS)

        order_words(
            g_codes[1][:].rearrange("p t g q -> p t (g q)"),
            g_raw_rest[:].rearrange("p g n -> p (g n)"),
        )
        for k in range(2):
            finish_right(0, k)
            store_right(0, k)
        for t in (0, 1):
            for g in range(M_GROUPS):
                multiply_g(2, t, g)
        for k in range(2):
            finish_right(1, k)
            store_right(1, k)
        copy_scaled(0)
        turn_h(0)
        copy_h(0)
        load_h(6)
        copy_scaled(1)
        for t in (2, 3):
            for g in range(M_GROUPS):
                multiply_g(2, t, g)
        turn_h(1)
        load_h(7)
        for k in range(2):
            finish_right(2, k)
        for k in range(2):
            store_right(2, k)
        sort_h(2)
        copy_h(1)
        quantize_scaled(0)
        turn_h(2)
        copy_h(2)
        sort_h(3)
        quantize_scaled(1)
        quantize_h(0)
        sort_h(4)
        copy_scaled(2)
        turn_h(3)
        multiply_h(0, (0, 1))
        copy_h(3)
        quantize_scaled(2)
        quantize_h(1)
        turn_h(4)
        multiply_h(0, (2,))
        quantize_h(2)
        sort_h(5)
        quantize_h(3)
        store_sketch(0)
        multiply_h(1)

        for u in range(5, UNITS):
            multiply_h(u - 3)
            store_sketch(u - 4)
            copy_h(u - 1)
            quantize_h(u - 1)
            turn_h(u)
            if u + 1 < UNITS:
                sort_h(u + 1)
        copy_h(UNITS - 1)
        quantize_h(UNITS - 1)
        store_sketch(UNITS - 4)
        for u in range(UNITS - 3, UNITS):
            multiply_h(u)
            store_sketch(u)
